import numpy as np
import ml_dtypes


def mxq(x, axis, fmt="e4m3"):
    dtype, down = {"e4m3": (ml_dtypes.float8_e4m3fn, 7), "e5m2": (ml_dtypes.float8_e5m2, 14)}[fmt]
    v = np.moveaxis(np.asarray(x, np.float32).astype(ml_dtypes.bfloat16).astype(np.float64), axis, -1)
    blocks = v.reshape(v.shape[:-1] + (-1, 32))
    amax = np.abs(blocks).max(-1, keepdims=True)
    byte = np.maximum(np.where(amax > 0, np.frexp(amax)[1] - 1 + 127, 0) - down, 1)
    scale = np.exp2(byte - 127.0)
    codes = (blocks / scale).astype(np.float32).astype(dtype).astype(np.float64)
    return np.moveaxis((codes * scale).reshape(v.shape), -1, axis)


WIDE = False


def mx_kscale(k):
    if not WIDE:
        return np.ones(k)
    levels = np.array([10, -10, 5, -5, 0])
    if k % 512:
        return np.exp2(np.random.permutation(np.resize(levels, k // 32))).repeat(32)
    a = np.empty((k // 512, 16))
    for p in range(k // 512):
        a[p, :8] = np.random.permutation(np.resize(levels, 8))
        for g in range(8):
            far = levels[np.abs(levels - a[p, g]) >= 10]
            a[p, g + 8] = far[np.random.randint(len(far))]
    return np.exp2(a.ravel()).repeat(32)


BF16 = ml_dtypes.bfloat16


def bf(x):
    return np.asarray(x, np.float32).astype(BF16)


def f64(x):
    return np.asarray(x).astype(np.float64)


E2M1 = np.array([0.0, 0.5, 1.0, 1.5, 2.0, 3.0, 4.0, 6.0, -0.0, -0.5, -1.0, -1.5, -2.0, -3.0, -4.0, -6.0])


def pack_weight(w, fmt):
    k, n = w.shape
    w = f64(bf(w)).reshape(k // 32, 32, n)
    amax = np.abs(w).max(1)
    if fmt == "e4m3":
        byte = np.frexp(amax)[1] - 1 + 127 - 7
    else:
        mant, ex = np.frexp(amax / 6.0)
        byte = np.where(mant > 0.5, ex, ex - 1) + 127
    byte = np.clip(np.where(amax > 0, byte, 1), 1, 254)
    scaled = (w * np.exp2(127.0 - byte)[:, None, :]).reshape(k, n).astype(np.float32)
    by_word = np.ascontiguousarray(scaled.reshape(k // 512, 128, 4, n).transpose(0, 1, 3, 2))
    if fmt == "e4m3":
        words = by_word.astype(ml_dtypes.float8_e4m3fn).view(np.uint8)
    else:
        c = by_word.astype(ml_dtypes.float4_e2m1fn).view(np.uint8) & 0xF
        words = c[..., 0::2] | (c[..., 1::2] << 4)
    return np.ascontiguousarray(words), np.ascontiguousarray(byte.astype(np.uint8).reshape(k // 512, 16, n))


def unpack_weight(words, scales, fmt):
    g, p, n, _ = words.shape
    if fmt == "e4m3":
        vals = np.ascontiguousarray(words).view(ml_dtypes.float8_e4m3fn).astype(np.float64)
    else:
        nib = np.empty((g, p, n, 4), np.uint8)
        nib[..., 0::2] = words & 0xF
        nib[..., 1::2] = words >> 4
        vals = E2M1[nib]
    vals = vals * np.repeat(np.exp2(scales.astype(np.float64) - 127.0), 8, axis=1)[..., None]
    return vals.transpose(0, 1, 3, 2).reshape(g * 512, n)
def pack4(w):
    words, scales = pack_weight(w, "e2m1")
    return words.reshape(words.shape[0], 128, -1), scales


def unpack4(words, scales):
    return unpack_weight(words.reshape(words.shape[0], 128, -1, 2), scales, "e2m1")


def planes(Y):
    n, m = Y.shape
    b = f64(bf(Y)).reshape(n // 32, 32, m)
    amax = np.abs(b).max(1)
    byte = np.clip(np.where(amax > 0, np.frexp(amax)[1] - 1 + 127 - 7, 1), 1, 254)
    codes = (b * np.exp2(127.0 - byte)[:, None, :]).reshape(n, m).astype(np.float32).astype(ml_dtypes.float8_e4m3fn).view(np.uint8)
    words = codes.reshape(n // 512, 128, 4, m).transpose(0, 1, 3, 2)
    return np.ascontiguousarray(words), np.ascontiguousarray(byte.astype(np.uint8).reshape(n // 512, 16, m))


M, K, F, N, A = 768, 1024, 4096, 512, 8

def setup_inputs():
    s = mx_kscale(K)
    t = mx_kscale(F)
    X = np.random.randn(K, M) * s[:, None]
    B = (0.5 * np.random.randn(K, 1) + 0.5 * np.random.randn(K, F)) / np.sqrt(K)
    x_words, x_scales = pack_weight(X, "e4m3")
    b_words, b_scales = pack4(B / s[:, None])
    w = np.exp(0.8 * np.random.randn(F // A, A))
    w = (w / w.sum(axis=1, keepdims=True)).reshape(F)
    g = np.exp(1.5 * np.random.randn(F, N))
    g = A * g / g.sum(axis=0, keepdims=True)
    return {"x_words": x_words, "x_scales": x_scales,
            "b_words": b_words, "b_scales": b_scales,
            "age_w": bf(w * t),
            "group_w": bf(g / t[:, None]),
            "background": bf(0.3 * np.exp(0.5 * np.random.randn(N))),
            "calibration": bf(np.exp(0.8 * np.random.randn(N))),
            "risk_time": bf(np.exp(0.3 * np.random.randn(M)))}

def reference(x_words, x_scales, b_words, b_scales, age_w, group_w, background, calibration, risk_time):
    X = unpack_weight(x_words, x_scales, "e4m3")
    B = unpack4(b_words, b_scales)
    H = np.exp(X.T @ B) * f64(age_w)
    S = mxq(H, 1, "e4m3") @ mxq(f64(group_w), 0, "e4m3")
    y = (S + f64(background)) * f64(calibration) * f64(risk_time)[:, None]
    words, scales = planes(y.T)
    return y, words, scales

@@ -1,0 +1,424 @@
+import math
+from contextlib import ExitStack
+
+import concourse.mybir as mybir
+from concourse.masks import make_identity
+
+M, K, F, N = 768, 1024, 4096, 512
+FLOPS = 2 * M * K * F + 2 * M * F * N
+
+F32 = mybir.dt.float32
+BF16 = mybir.dt.bfloat16
+I32 = mybir.dt.int32
+U32 = mybir.dt.uint32
+U8 = mybir.dt.uint8
+FP8X4 = mybir.dt.float8_e4m3fn_x4
+FP4X4 = mybir.dt.float4_e2m1fn_x4
+ALU = mybir.AluOpType
+ACT = mybir.ActivationFunctionType
+
+P = 128
+PACK = 4
+PASS = P * PACK
+K_PASSES = K // PASS
+F_PASSES = F // PASS
+CHUNKS = ((0, 512), (512, 256))
+EARLY_NARROW = 7
+PARTS = ((0, 2), (2, 3), (5, 3))
+DRAIN_V = ((1, 3), (1, 3))
+Y_V = (1, 3, 5)
+CATCH = 2
+Y_STEPS = (2, 2, 3, 3)
+LOADS = "b0 x0 s0 xs b1 g0 s1 b2 g1 x1 b3 g2 s2 b4 g3 b5 g4 c b6 g5 b7 g6 g7"
+SCALAR_SHARE = (192, 64)
+LATE_SHARE = (0, 64)
+FILL_LEAD = 3
+FILL_RATE = (2, 2)
+WORK_BUFS = 2
+XS_QUEUE = "s"
+FIRST_NARROW = 0
+PY_STEPS = (3, 4)
+PL_STEP = 4
+LATE_FROM = 0
+ZERO_WEIGHT_LOG = -1.0e30
+
+
+def tile_weighted_region_expected_events_h2_kernel(
+    tc, x_words, x_scales, b_words, b_scales, age_w, group_w, background, calibration, risk_time, out_0, out_1, out_2
+):
+    nc = tc.nc
+    with ExitStack() as ctx:
+        keep = ctx.enter_context(tc.tile_pool(name="keep", bufs=1))
+        work = ctx.enter_context(tc.tile_pool(name="work", bufs=WORK_BUFS))
+        ring = ctx.enter_context(tc.psum_pool(name="ring", bufs=4))
+        sums = ctx.enter_context(tc.psum_pool(name="sums", bufs=1))
+        ctx.enter_context(tc.manual_schedule())
+
+        def kept(shape, dtype, name):
+            return keep.tile(shape, dtype, name=name, align_bytes=64)
+
+        x_codes = [kept([P, K_PASSES, w], U32, "x_codes%d" % c) for c, (m0, w) in enumerate(CHUNKS)]
+        x_plane = kept([P, K_PASSES, M], U8, "x_plane")
+        parts = PARTS
+        b_plane_raw = [kept([P, K_PASSES, n * PASS], U8, "b_plane_raw%d" % i) for i, (g0, n) in enumerate(parts)]
+        b_plane = [kept([P, K_PASSES, PASS], U8, "b_plane%d" % g) for g in range(F_PASSES)]
+        b_raw = [kept([P, K_PASSES, 2 * PASS], U8, "b_raw%d" % g) for g in range(F_PASSES)]
+        b_codes = [kept([P, K_PASSES, 2 * PASS], U8, "b_codes%d" % g) for g in range(F_PASSES)]
+        g_raw = [kept([P, PACK, N], BF16, "g_raw%d" % g) for g in range(F_PASSES)]
+        g_codes = [kept([P, N], U32, "g_codes%d" % g) for g in range(F_PASSES)]
+        g_plane = [kept([P, N], U8, "g_plane%d" % g) for g in range(F_PASSES)]
+        rows = kept([P, PASS], BF16, "rows")
+        rows32 = kept([P, PACK, P], F32, "rows32")
+        rt_rows = kept([P, P], BF16, "rt_rows")
+        rt_rows32 = kept([P, P], F32, "rt_rows32")
+        ident = kept([P, P], F32, "ident")
+        warm = kept([P, 1], F32, "warm")
+        warm_out = kept([P, 1], F32, "warm_out")
+        cal_bf = kept([P, PACK], BF16, "cal_bf")
+        bg_bf = kept([P, PACK], BF16, "bg_bf")
+        cal = kept([P, PACK], F32, "cal")
+        bg = kept([P, PACK], F32, "bg")
+        bg_cal = kept([P, PACK], F32, "bg_cal")
+        rt_row = kept([P, M], BF16, "rt_row")
+        rt_col = kept([P, M // P], F32, "rt_col")
+        w_col = kept([P, PACK, F_PASSES], F32, "w_col")
+        w_expo = kept([P, PACK, F_PASSES], I32, "w_expo")
+        w_frac = kept([P, PACK, F_PASSES], I32, "w_frac")
+        w_mant = kept([P, PACK, F_PASSES], F32, "w_mant")
+        ln_mant = kept([P, PACK, F_PASSES], F32, "ln_mant")
+        ln_expo = kept([P, PACK, F_PASSES], F32, "ln_expo")
+        ln_zero = kept([P, PACK, F_PASSES], F32, "ln_zero")
+        ln_rest = kept([P, PACK, F_PASSES], F32, "ln_rest")
+        ln_w = kept([P, PACK, F_PASSES], F32, "ln_w")
+        w_neg = kept([P, PACK, F_PASSES], F32, "w_neg")
+        w_sign = kept([P, PACK, F_PASSES], F32, "w_sign")
+
+        def load_x(c):
+            m0, w = CHUNKS[c]
+            src = x_words.rearrange("g p m t -> p g (m t)")[:, :, PACK * m0 : PACK * (m0 + w)]
+            nc.sync.dma_start(out=x_codes[c][:].bitcast(I32), in_=src.bitcast(I32))
+
+        def load_plane(plane, scales, queue):
+            for q in range(4):
+                src = scales[:, 4 * q : 4 * q + 4, :].rearrange("g r n -> r g n")
+                queue.dma_start(out=plane[32 * q : 32 * q + 4, :, :].bitcast(I32), in_=src.bitcast(I32))
+
+        def load_b_plane(i):
+            g0, n = parts[i]
+            load_plane(b_plane_raw[i], b_scales[:, :, g0 * PASS : (g0 + n) * PASS], nc.sync)
+
+        def load_b(g):
+            src = b_words.rearrange("k p n -> p k n")[:, :, 2 * PASS * g : 2 * PASS * (g + 1)]
+            nc.sync.dma_start(out=b_raw[g][:].bitcast(I32), in_=src.bitcast(I32))
+
+        def load_g(g):
+            src = group_w[PASS * g : PASS * (g + 1), :].rearrange("(v t r) n -> r v t n", t=PACK, r=4)
+            for r in range(4):
+                nc.sync.dma_start(out=g_raw[g][r:P:4, :, :], in_=src[r])
+
+        nc.vector.memset(b_plane_raw[0][:].bitcast(I32), 0)
+        if XS_QUEUE == "g":
+            nc.gpsimd.memset(x_plane[:].bitcast(I32), 0)
+        else:
+            nc.vector.memset(x_plane[:].bitcast(I32), 0)
+        nc.vector.memset(warm[:], 1.0)
+        nc.vector.memset(rows32[:], 0.0)
+        make_identity(nc, ident[:])
+        if XS_QUEUE == "g":
+            load_plane(x_plane, x_scales, nc.gpsimd)
+        for plane in b_plane_raw[1:]:
+            nc.vector.memset(plane[:].bitcast(I32), 0)
+        nc.vector.memset(rt_rows32[:], 0.0)
+
+        nc.scalar.dma_start(out=rows[0:F_PASSES, :], in_=age_w.rearrange("(g f) -> g f", f=PASS))
+        nc.scalar.activation(out=warm_out[:], in_=warm[:], func=ACT.Ln)
+
+        for item in LOADS.split():
+            if item == "xs":
+                if XS_QUEUE != "g":
+                    load_plane(x_plane, x_scales, nc.sync)
+            elif item == "c":
+                nc.sync.dma_start(out=cal_bf[:], in_=calibration.rearrange("(p t) -> p t", t=PACK))
+                nc.sync.dma_start(out=bg_bf[:], in_=background.rearrange("(p t) -> p t", t=PACK))
+                nc.sync.dma_start(out=rt_rows[0 : M // P, :], in_=risk_time.rearrange("(j p) -> j p", p=P))
+                nc.sync.dma_start(out=rt_row[:], in_=risk_time.partition_broadcast(P))
+            else:
+                {"b": load_b, "x": load_x, "s": load_b_plane, "g": load_g}[item[0]](int(item[1]))
+
+        nc.vector.tensor_copy(
+            out=rows32[0:F_PASSES, :, :].rearrange("g t (v r) -> g t v r", r=4),
+            in_=rows[0:F_PASSES, :].rearrange("g (v t r) -> g t v r", t=PACK, r=4),
+        )
+        turned = ring.tile([P, PACK, P], F32, name="turned", tag="ring")
+        for t in range(PACK):
+            nc.tensor.transpose(turned[:, t, :], rows32[:, t, :], ident[:])
+        nc.vector.tensor_copy(out=w_col[:], in_=turned[:, :, 0:F_PASSES])
+        w_bits = w_col[:].bitcast(I32)
+        nc.vector.tensor_scalar(
+            out=w_frac[:], in0=w_bits, scalar1=16, scalar2=127, op0=ALU.logical_shift_right, op1=ALU.bitwise_and
+        )
+        nc.vector.tensor_scalar(
+            out=w_expo[:], in0=w_bits, scalar1=23, scalar2=255, op0=ALU.logical_shift_right, op1=ALU.bitwise_and
+        )
+        nc.vector.tensor_scalar(
+            out=w_mant[:], in0=w_frac[:], scalar1=1.0 / 128, scalar2=1.0, op0=ALU.mult, op1=ALU.add
+        )
+        nc.scalar.activation(out=ln_mant[:], in_=w_mant[:], func=ACT.Ln)
+        nc.scalar.activation(out=warm_out[:], in_=warm[:], func=ACT.Exp)
+        nc.vector.tensor_scalar(
+            out=ln_expo[:], in0=w_expo[:], scalar1=-127.0, scalar2=math.log(2.0), op0=ALU.add, op1=ALU.mult
+        )
+        nc.vector.tensor_scalar(
+            out=ln_zero[:], in0=w_expo[:], scalar1=0.0, scalar2=ZERO_WEIGHT_LOG, op0=ALU.is_equal, op1=ALU.mult
+        )
+        nc.vector.tensor_scalar(out=w_neg[:], in0=w_col[:], scalar1=0.0, scalar2=-2.0, op0=ALU.is_lt, op1=ALU.mult)
+
+        def order_b(g):
+            i = max(j for j, (g0, n) in enumerate(parts) if g0 <= g)
+            g0 = parts[i][0]
+            nc.vector.tensor_copy(
+                out=b_codes[g][:].bitcast(I32).rearrange("p k (t v e) -> p k t v e", t=PACK, e=2),
+                in_=b_raw[g][:].bitcast(I32).rearrange("p k (v t e) -> p k t v e", t=PACK, e=2),
+            )
+            src = b_plane_raw[i][:, :, (g - g0) * PASS : (g - g0 + 1) * PASS]
+            nc.vector.tensor_copy(
+                out=b_plane[g][:].bitcast(I32).rearrange("p k (t v) -> p k v t", t=PACK),
+                in_=src.bitcast(I32).rearrange("p k (v t) -> p k v t", t=PACK),
+            )
+
+        rates, rates_packed, h_codes, h_plane, g_packed, acc, scaled = {}, {}, {}, {}, {}, {}, {}
+
+        def stage1(c, g, between):
+            m0, w = CHUNKS[c]
+            rates[c, g] = work.tile([P, PACK, w], BF16, name="rates", tag="rates%d" % c, align_bytes=64)
+            per_bank = 512 // w
+            n = 512 if w == 512 else 128
+            for t0 in range(0, PACK, per_bank):
+                bank = ring.tile([P, per_bank, w], F32, name="bank", tag="ring")
+                for t in range(t0, t0 + per_bank):
+                    for h in range(0, w, n):
+                        for k in range(K_PASSES):
+                            nc.tensor.matmul_mx(
+                                out=bank[:, t - t0, h : h + n],
+                                lhsT=b_codes[g][:, k, 2 * P * t : 2 * P * (t + 1)].bitcast(FP4X4),
+                                lhsT_scale=b_plane[g][:, k, P * t : P * (t + 1)],
+                                rhs=x_codes[c][:, k, h : h + n].bitcast(FP8X4),
+                                rhs_scale=x_plane[:, k, m0 + h : m0 + h + n],
+                                start=(k == 0),
+                                stop=(k == K_PASSES - 1),
+                            )
+                for t in range(t0, t0 + per_bank):
+                    nc.scalar.activation(
+                        out=rates[c, g][:, t, :], in_=bank[:, t - t0, :], func=ACT.Exp, bias=ln_w[:, t, g : g + 1]
+                    )
+                    if t == 0:
+                        between()
+
+        def pack_rates(c, g, copy, lo, hi):
+            if (c, g) not in rates_packed:
+                rates_packed[c, g] = work.tile(
+                    [P, CHUNKS[c][1], PACK], BF16, name="rates_packed", tag="packed%d" % c, align_bytes=64
+                )
+            if lo < hi:
+                copy(
+                    out=rates_packed[c, g][:, lo:hi, :].rearrange("p (a i) t -> p a t i", i=4),
+                    in_=rates[c, g][:, :, lo:hi].rearrange("p t (a i) -> p a t i", i=4),
+                )
+
+        def quantize_rates(c, g):
+            w = CHUNKS[c][1]
+            h_codes[c, g] = kept([P, w], U32, "h_codes%d_%d" % (c, g))
+            h_plane[c, g] = kept([P, w], U8, "h_plane%d_%d" % (c, g))
+            nc.vector.quantize_mx(
+                out=h_codes[c, g][:].bitcast(FP8X4),
+                scales=h_plane[c, g][:],
+                in_=rates_packed[c, g][:].rearrange("p m t -> p (m t)"),
+            )
+
+        def sign_g(g):
+            for t in range(PACK):
+                nc.vector.tensor_scalar(
+                    out=g_raw[g][:, t, :], in0=g_raw[g][:, t, :], scalar1=w_sign[:, t, g : g + 1], scalar2=None, op0=ALU.mult
+                )
+
+        def pack_g(g):
+            g_packed[g] = work.tile([P, PACK, P, PACK], BF16, name="g_packed", align_bytes=64)
+            nc.vector.tensor_copy(
+                out=g_packed[g][:].rearrange("p s a t -> p a t s"),
+                in_=g_raw[g][:].rearrange("p t (a s) -> p a t s", s=PACK),
+            )
+
+        def quantize_g(g):
+            nc.vector.quantize_mx(
+                out=g_codes[g][:].bitcast(FP8X4),
+                scales=g_plane[g][:],
+                in_=g_packed[g][:].rearrange("p s a t -> p (s a t)"),
+            )
+
+        def stage2(c, g):
+            w = CHUNKS[c][1]
+            for s in range(PACK):
+                if g == 0:
+                    acc[c, s] = sums.tile([P, w], F32, name="acc", tag="acc%d" % s)
+                nc.tensor.matmul_mx(
+                    out=acc[c, s][:],
+                    lhsT=g_codes[g][:, P * s : P * (s + 1)].bitcast(FP8X4),
+                    lhsT_scale=g_plane[g][:, P * s : P * (s + 1)],
+                    rhs=h_codes[c, g][:].bitcast(FP8X4),
+                    rhs_scale=h_plane[c, g][:],
+                    start=(g == 0),
+                    stop=(g == F_PASSES - 1),
+                )
+
+        def drain(c, on_vector):
+            w = CHUNKS[c][1]
+            scaled[c] = kept([P, PACK, w], F32, "scaled%d" % c)
+            for s in range(PACK):
+                if s in on_vector:
+                    nc.vector.tensor_scalar(
+                        out=scaled[c][:, s, :], in0=acc[c, s][:], scalar1=bg[:, s : s + 1], scalar2=cal[:, s : s + 1],
+                        op0=ALU.add, op1=ALU.mult,
+                    )
+                else:
+                    nc.scalar.activation(
+                        out=scaled[c][:, s, :], in_=acc[c, s][:], func=ACT.Identity,
+                        scale=cal[:, s : s + 1], bias=bg_cal[:, s : s + 1],
+                    )
+
+        y_packed = {}
+
+        def pack_y(c, lo, hi):
+            m0, w = CHUNKS[c]
+            if c not in y_packed:
+                y_packed[c] = kept([P, w, PACK], BF16, "y_packed%d" % c)
+            nc.vector.tensor_tensor(
+                out=y_packed[c][:, lo:hi, :].rearrange("p (a i) s -> p a s i", i=4),
+                in0=scaled[c][:, :, lo:hi].rearrange("p s (a i) -> p a s i", i=4),
+                in1=rt_row[:, m0 + lo : m0 + hi]
+                .rearrange("p (a i) -> p a i", i=4)
+                .unsqueeze(2)
+                .to_broadcast([P, (hi - lo) // 4, PACK, 4]),
+                op=ALU.mult,
+            )
+
+        def turn_rt():
+            bank = ring.tile([P, P], F32, name="bank", tag="ring")
+            nc.tensor.transpose(bank[:], rt_rows32[:], ident[:])
+            nc.vector.tensor_copy(out=rt_col[:], in_=bank[:, 0 : M // P])
+
+        def store_planes(c):
+            m0, w = CHUNKS[c]
+            y_codes = kept([P, w], U32, "y_codes%d" % c)
+            y_plane = kept([P, w], U8, "y_plane%d" % c)
+            nc.vector.quantize_mx(
+                out=y_codes[:].bitcast(FP8X4), scales=y_plane[:], in_=y_packed[c][:].rearrange("p m s -> p (m s)")
+            )
+            dst = out_1[0].rearrange("p m t -> p (m t)")[:, PACK * m0 : PACK * (m0 + w)]
+            nc.sync.dma_start(out=dst.bitcast(I32), in_=y_codes[:].bitcast(I32))
+            for q in range(4):
+                nc.sync.dma_start(
+                    out=out_2[0, 4 * q : 4 * q + 4, m0 : m0 + w].bitcast(I32),
+                    in_=y_plane[32 * q : 32 * q + 4, :].bitcast(I32),
+                )
+
+        def store_y(c, j):
+            m0 = CHUNKS[c][0]
+            bank = ring.tile([P, PACK, P], F32, name="bank", tag="ring")
+            for s in range(PACK):
+                nc.tensor.transpose(bank[:, s, :], scaled[c][:, s, P * j : P * (j + 1)], ident[:])
+            row = m0 // P + j
+            y = kept([P, P, PACK], F32, "y%d" % row)
+            if row in Y_V:
+                nc.vector.tensor_scalar(
+                    out=y[:], in0=bank[:].rearrange("m s p -> m p s"), scalar1=rt_col[:, row : row + 1], scalar2=None, op0=ALU.mult
+                )
+            else:
+                nc.scalar.activation(
+                    out=y[:], in_=bank[:].rearrange("m s p -> m p s"), func=ACT.Copy, scale=rt_col[:, row : row + 1]
+                )
+            nc.sync.dma_start(out=out_0[P * row : P * (row + 1), :], in_=y[:].rearrange("m p s -> m (p s)"))
+
+        units = []
+        for g in range(F_PASSES):
+            if FIRST_NARROW and g < EARLY_NARROW:
+                units.append((1, g))
+            units.append((0, g))
+            if not FIRST_NARROW and 1 <= g <= EARLY_NARROW:
+                units.append((1, g - 1))
+        last_wide = units.index((0, F_PASSES - 1))
+        units += [(1, g) for g in range(EARLY_NARROW, F_PASSES)]
+
+        order_b(0)
+        nc.vector.tensor_tensor(out=ln_rest[:], in0=ln_expo[:], in1=ln_zero[:], op=ALU.add)
+        nc.vector.tensor_scalar(out=w_sign[:], in0=w_neg[:], scalar1=1.0, scalar2=None, op0=ALU.add)
+        nc.vector.tensor_tensor(out=ln_w[:], in0=ln_rest[:], in1=ln_mant[:], op=ALU.add)
+        order_b(1)
+
+        fillers = []
+        for g in range(F_PASSES + 1):
+            if g < F_PASSES:
+                fillers.append((sign_g, g))
+            if g >= 1:
+                fillers.append((quantize_g, g - 1))
+            if g + 2 < F_PASSES:
+                fillers.append((order_b, g + 2))
+            if g < F_PASSES:
+                fillers.append((pack_g, g))
+
+        def fill(count):
+            for step, g in fillers[:count]:
+                step(g)
+            fillers[:count] = []
+
+        narrow_done = 0
+        fill(FILL_LEAD)
+        for i in range(len(units) + 2):
+            now = units[i] if i < len(units) else None
+            prev = units[i - 1] if 1 <= i <= len(units) else None
+            prev2 = units[i - 2] if i >= 2 else None
+            share = (SCALAR_SHARE if i < last_wide + LATE_FROM else LATE_SHARE)[prev[0]] if prev else 0
+
+            def scalar_share():
+                if prev:
+                    pack_rates(*prev, nc.scalar.copy, 0, share)
+
+            if now:
+                stage1(*now, scalar_share)
+            else:
+                scalar_share()
+            count = FILL_RATE[now[0]] if now else 0
+            if prev:
+                pack_rates(*prev, nc.vector.tensor_copy, share, CHUNKS[prev[0]][1])
+            fill((count + 1) // 2)
+            if prev:
+                quantize_rates(*prev)
+            fill(count // 2)
+            if i == last_wide:
+                nc.vector.tensor_copy(out=cal[:], in_=cal_bf[:])
+                nc.vector.tensor_copy(out=bg[:], in_=bg_bf[:])
+                nc.vector.tensor_copy(out=rt_rows32[0 : M // P, :], in_=rt_rows[0 : M // P, :])
+                nc.vector.tensor_tensor(out=bg_cal[:], in0=cal_bf[:], in1=bg_bf[:], op=ALU.mult)
+            if prev2 and prev2[0] == 0:
+                stage2(*prev2)
+            if i == last_wide + 2:
+                drain(0, DRAIN_V[0])
+            for j in range(2):
+                if i == last_wide + PY_STEPS[j]:
+                    pack_y(0, 256 * j, 256 * (j + 1))
+            if i == last_wide + PL_STEP:
+                store_planes(0)
+            if i == last_wide + Y_STEPS[0]:
+                turn_rt()
+            for j in range(4):
+                if i == last_wide + Y_STEPS[j]:
+                    store_y(0, j)
+            if i >= last_wide + 2:
+                ready = [g for g in range(narrow_done, F_PASSES) if (1, g) in units[: i - 1]]
+                for g in ready if i == len(units) + 1 else ready[:CATCH]:
+                    stage2(1, g)
+                    narrow_done += 1
+        drain(1, DRAIN_V[1])
+        pack_y(1, 0, 256)
+        for j in range(2):
+            store_y(1, j)
+        store_planes(1)

@@ -20,27 +20,28 @@ ACT = mybir.ActivationFunctionType
 P = 128
 PACK = 4
 PASS = P * PACK
+BANK = 512
+RUN = 4
+QUADRANTS = 4
 K_PASSES = K // PASS
-F_PASSES = F // PASS
+GROUPS = F // PASS
+WIDE, NARROW = 0, 1
 CHUNKS = ((0, 512), (512, 256))
-EARLY_NARROW = 7
-PARTS = ((0, 2), (2, 3), (5, 3))
-DRAIN_V = ((1, 3), (1, 3))
-Y_V = (1, 3, 5)
-CATCH = 2
-Y_STEPS = (2, 2, 3, 3)
-LOADS = "b0 x0 s0 xs b1 g0 s1 b2 g1 x1 b3 g2 s2 b4 g3 b5 g4 c b6 g5 b7 g6 g7"
-SCALAR_SHARE = (192, 64)
-LATE_SHARE = (0, 64)
-FILL_LEAD = 3
-FILL_RATE = (2, 2)
-WORK_BUFS = 2
-XS_QUEUE = "s"
-FIRST_NARROW = 0
-PY_STEPS = (3, 4)
-PL_STEP = 4
-LATE_FROM = 0
+STAGE1_N = (512, 128)
 ZERO_WEIGHT_LOG = -1.0e30
+
+B_PLANE_PARTS = ((0, 2), (2, 3), (5, 3))
+LOADS = "b0 s0 x0 p b1 g0 s1 b2 g1 x1 r b3 g2 s2 b4 g3 b5 g4 c b6 g5 b7 g6 g7"
+
+EARLY_WIDE, EARLY_NARROW = 3, 4
+NARROW_PACK_STEP = (11, 12, 13, 14, 14, 15, 16, 17)
+WIDE_STAGE2_STEP = (6, 9, 10, 11, 12, 14, 15, 15)
+SCALAR_COLUMNS = ((128, 128, 256, 256, 256, 256, 256, 256), (64, 64, 64, 64, 0, 0, 0, 0))
+FILL_AHEAD = 3
+RISK_STEP = 10
+NARROW_PASSES_A_STEP = 4
+STEPS = 19
+WARM_PASSES = (5, 14)
 
 
 def tile_weighted_region_expected_events_h2_kernel(
@@ -49,7 +50,7 @@ def tile_weighted_region_expected_events_h2_kernel(
     nc = tc.nc
     with ExitStack() as ctx:
         keep = ctx.enter_context(tc.tile_pool(name="keep", bufs=1))
-        work = ctx.enter_context(tc.tile_pool(name="work", bufs=WORK_BUFS))
+        work = ctx.enter_context(tc.tile_pool(name="work", bufs=3))
         ring = ctx.enter_context(tc.psum_pool(name="ring", bufs=4))
         sums = ctx.enter_context(tc.psum_pool(name="sums", bufs=1))
         ctx.enter_context(tc.manual_schedule())
@@ -57,188 +58,101 @@ def tile_weighted_region_expected_events_h2_kernel(
         def kept(shape, dtype, name):
             return keep.tile(shape, dtype, name=name, align_bytes=64)
 
+        def per_cell(dtype, name):
+            return kept([P, PACK, GROUPS], dtype, name)
+
         x_codes = [kept([P, K_PASSES, w], U32, "x_codes%d" % c) for c, (m0, w) in enumerate(CHUNKS)]
         x_plane = kept([P, K_PASSES, M], U8, "x_plane")
-        parts = PARTS
-        b_plane_raw = [kept([P, K_PASSES, n * PASS], U8, "b_plane_raw%d" % i) for i, (g0, n) in enumerate(parts)]
-        b_plane = [kept([P, K_PASSES, PASS], U8, "b_plane%d" % g) for g in range(F_PASSES)]
-        b_raw = [kept([P, K_PASSES, 2 * PASS], U8, "b_raw%d" % g) for g in range(F_PASSES)]
-        b_codes = [kept([P, K_PASSES, 2 * PASS], U8, "b_codes%d" % g) for g in range(F_PASSES)]
-        g_raw = [kept([P, PACK, N], BF16, "g_raw%d" % g) for g in range(F_PASSES)]
-        g_codes = [kept([P, N], U32, "g_codes%d" % g) for g in range(F_PASSES)]
-        g_plane = [kept([P, N], U8, "g_plane%d" % g) for g in range(F_PASSES)]
-        rows = kept([P, PASS], BF16, "rows")
-        rows32 = kept([P, PACK, P], F32, "rows32")
+        b_plane_raw = [
+            kept([P, K_PASSES, n * PASS], U8, "b_plane_raw%d" % i) for i, (g0, n) in enumerate(B_PLANE_PARTS)
+        ]
+        b_plane = [kept([P, K_PASSES, PASS], U8, "b_plane%d" % g) for g in range(GROUPS)]
+        b_codes = [kept([P, K_PASSES, 2 * PASS], U8, "b_codes%d" % g) for g in range(GROUPS)]
+        g_codes = [kept([P, N], U32, "g_codes%d" % g) for g in range(GROUPS)]
+        g_plane = [kept([P, N], U8, "g_plane%d" % g) for g in range(GROUPS)]
+        w_rows = kept([P, PASS], BF16, "w_rows")
+        w_rows32 = kept([P, PACK, P], F32, "w_rows32")
         rt_rows = kept([P, P], BF16, "rt_rows")
         rt_rows32 = kept([P, P], F32, "rt_rows32")
         ident = kept([P, P], F32, "ident")
-        warm = kept([P, 1], F32, "warm")
-        warm_out = kept([P, 1], F32, "warm_out")
+        one = kept([P, 1], F32, "one")
+        unused = kept([P, 1], F32, "unused")
         cal_bf = kept([P, PACK], BF16, "cal_bf")
         bg_bf = kept([P, PACK], BF16, "bg_bf")
         cal = kept([P, PACK], F32, "cal")
         bg = kept([P, PACK], F32, "bg")
         bg_cal = kept([P, PACK], F32, "bg_cal")
-        rt_row = kept([P, M], BF16, "rt_row")
-        rt_col = kept([P, M // P], F32, "rt_col")
-        w_col = kept([P, PACK, F_PASSES], F32, "w_col")
-        w_expo = kept([P, PACK, F_PASSES], I32, "w_expo")
-        w_frac = kept([P, PACK, F_PASSES], I32, "w_frac")
-        w_mant = kept([P, PACK, F_PASSES], F32, "w_mant")
-        ln_mant = kept([P, PACK, F_PASSES], F32, "ln_mant")
-        ln_expo = kept([P, PACK, F_PASSES], F32, "ln_expo")
-        ln_zero = kept([P, PACK, F_PASSES], F32, "ln_zero")
-        ln_rest = kept([P, PACK, F_PASSES], F32, "ln_rest")
-        ln_w = kept([P, PACK, F_PASSES], F32, "ln_w")
-        w_neg = kept([P, PACK, F_PASSES], F32, "w_neg")
-        w_sign = kept([P, PACK, F_PASSES], F32, "w_sign")
+        rt_along_free = kept([P, M], BF16, "rt_along_free")
+        rt_on_partitions = kept([P, M // P], F32, "rt_on_partitions")
+        w_col = per_cell(F32, "w_col")
+        w_expo = per_cell(I32, "w_expo")
+        w_frac = per_cell(I32, "w_frac")
+        w_mant = per_cell(F32, "w_mant")
+        ln_mant = per_cell(F32, "ln_mant")
+        ln_expo = per_cell(F32, "ln_expo")
+        ln_zero = per_cell(F32, "ln_zero")
+        ln_rest = per_cell(F32, "ln_rest")
+        ln_w = per_cell(F32, "ln_w")
+        w_neg = per_cell(F32, "w_neg")
+        w_sign = per_cell(F32, "w_sign")
+        zeros = kept([P, PASS], BF16, "zeros")
+        zero_codes = kept([P, P], U32, "zero_codes")
+        zero_plane = kept([P, P], U8, "zero_plane")
+        b_raw, g_raw, g_packed = {}, {}, {}
+        rates, rates_packed, h_codes, h_plane = {}, {}, {}, {}
+        acc, scaled, y_packed = {}, {}, {}
 
         def load_x(c):
             m0, w = CHUNKS[c]
-            src = x_words.rearrange("g p m t -> p g (m t)")[:, :, PACK * m0 : PACK * (m0 + w)]
+            src = x_words.rearrange("k p m t -> p k (m t)")[:, :, PACK * m0 : PACK * (m0 + w)]
             nc.sync.dma_start(out=x_codes[c][:].bitcast(I32), in_=src.bitcast(I32))
 
-        def load_plane(plane, scales, queue):
-            for q in range(4):
-                src = scales[:, 4 * q : 4 * q + 4, :].rearrange("g r n -> r g n")
-                queue.dma_start(out=plane[32 * q : 32 * q + 4, :, :].bitcast(I32), in_=src.bitcast(I32))
+        def load_plane(plane, scales):
+            for q in range(QUADRANTS):
+                src = scales[:, 4 * q : 4 * q + 4, :].rearrange("k r n -> r k n")
+                nc.sync.dma_start(out=plane[32 * q : 32 * q + 4, :, :].bitcast(I32), in_=src.bitcast(I32))
 
         def load_b_plane(i):
-            g0, n = parts[i]
-            load_plane(b_plane_raw[i], b_scales[:, :, g0 * PASS : (g0 + n) * PASS], nc.sync)
+            g0, n = B_PLANE_PARTS[i]
+            load_plane(b_plane_raw[i], b_scales[:, :, g0 * PASS : (g0 + n) * PASS])
 
         def load_b(g):
+            b_raw[g] = work.tile([P, K_PASSES, 2 * PASS], U8, name="b_raw", bufs=4, align_bytes=64)
             src = b_words.rearrange("k p n -> p k n")[:, :, 2 * PASS * g : 2 * PASS * (g + 1)]
             nc.sync.dma_start(out=b_raw[g][:].bitcast(I32), in_=src.bitcast(I32))
 
         def load_g(g):
+            g_raw[g] = work.tile([P, PACK, N], BF16, name="g_raw", bufs=6, align_bytes=64)
             src = group_w[PASS * g : PASS * (g + 1), :].rearrange("(v t r) n -> r v t n", t=PACK, r=4)
             for r in range(4):
                 nc.sync.dma_start(out=g_raw[g][r:P:4, :, :], in_=src[r])
 
-        nc.vector.memset(b_plane_raw[0][:].bitcast(I32), 0)
-        if XS_QUEUE == "g":
-            nc.gpsimd.memset(x_plane[:].bitcast(I32), 0)
-        else:
-            nc.vector.memset(x_plane[:].bitcast(I32), 0)
-        nc.vector.memset(warm[:], 1.0)
-        nc.vector.memset(rows32[:], 0.0)
-        make_identity(nc, ident[:])
-        if XS_QUEUE == "g":
-            load_plane(x_plane, x_scales, nc.gpsimd)
-        for plane in b_plane_raw[1:]:
-            nc.vector.memset(plane[:].bitcast(I32), 0)
-        nc.vector.memset(rt_rows32[:], 0.0)
-
-        nc.scalar.dma_start(out=rows[0:F_PASSES, :], in_=age_w.rearrange("(g f) -> g f", f=PASS))
-        nc.scalar.activation(out=warm_out[:], in_=warm[:], func=ACT.Ln)
-
-        for item in LOADS.split():
-            if item == "xs":
-                if XS_QUEUE != "g":
-                    load_plane(x_plane, x_scales, nc.sync)
-            elif item == "c":
-                nc.sync.dma_start(out=cal_bf[:], in_=calibration.rearrange("(p t) -> p t", t=PACK))
-                nc.sync.dma_start(out=bg_bf[:], in_=background.rearrange("(p t) -> p t", t=PACK))
-                nc.sync.dma_start(out=rt_rows[0 : M // P, :], in_=risk_time.rearrange("(j p) -> j p", p=P))
-                nc.sync.dma_start(out=rt_row[:], in_=risk_time.partition_broadcast(P))
-            else:
-                {"b": load_b, "x": load_x, "s": load_b_plane, "g": load_g}[item[0]](int(item[1]))
-
-        nc.vector.tensor_copy(
-            out=rows32[0:F_PASSES, :, :].rearrange("g t (v r) -> g t v r", r=4),
-            in_=rows[0:F_PASSES, :].rearrange("g (v t r) -> g t v r", t=PACK, r=4),
-        )
-        turned = ring.tile([P, PACK, P], F32, name="turned", tag="ring")
-        for t in range(PACK):
-            nc.tensor.transpose(turned[:, t, :], rows32[:, t, :], ident[:])
-        nc.vector.tensor_copy(out=w_col[:], in_=turned[:, :, 0:F_PASSES])
-        w_bits = w_col[:].bitcast(I32)
-        nc.vector.tensor_scalar(
-            out=w_frac[:], in0=w_bits, scalar1=16, scalar2=127, op0=ALU.logical_shift_right, op1=ALU.bitwise_and
-        )
-        nc.vector.tensor_scalar(
-            out=w_expo[:], in0=w_bits, scalar1=23, scalar2=255, op0=ALU.logical_shift_right, op1=ALU.bitwise_and
-        )
-        nc.vector.tensor_scalar(
-            out=w_mant[:], in0=w_frac[:], scalar1=1.0 / 128, scalar2=1.0, op0=ALU.mult, op1=ALU.add
-        )
-        nc.scalar.activation(out=ln_mant[:], in_=w_mant[:], func=ACT.Ln)
-        nc.scalar.activation(out=warm_out[:], in_=warm[:], func=ACT.Exp)
-        nc.vector.tensor_scalar(
-            out=ln_expo[:], in0=w_expo[:], scalar1=-127.0, scalar2=math.log(2.0), op0=ALU.add, op1=ALU.mult
-        )
-        nc.vector.tensor_scalar(
-            out=ln_zero[:], in0=w_expo[:], scalar1=0.0, scalar2=ZERO_WEIGHT_LOG, op0=ALU.is_equal, op1=ALU.mult
-        )
-        nc.vector.tensor_scalar(out=w_neg[:], in0=w_col[:], scalar1=0.0, scalar2=-2.0, op0=ALU.is_lt, op1=ALU.mult)
+        def load_epilogue_vectors():
+            nc.sync.dma_start(out=cal_bf[:], in_=calibration.rearrange("(p s) -> p s", s=PACK))
+            nc.sync.dma_start(out=bg_bf[:], in_=background.rearrange("(p s) -> p s", s=PACK))
+            nc.sync.dma_start(out=rt_along_free[:], in_=risk_time.partition_broadcast(P))
 
         def order_b(g):
-            i = max(j for j, (g0, n) in enumerate(parts) if g0 <= g)
-            g0 = parts[i][0]
+            part = max(i for i, (g0, n) in enumerate(B_PLANE_PARTS) if g0 <= g)
+            first = (g - B_PLANE_PARTS[part][0]) * PASS
+            raw_scales = b_plane_raw[part][:, :, first : first + PASS]
             nc.vector.tensor_copy(
                 out=b_codes[g][:].bitcast(I32).rearrange("p k (t v e) -> p k t v e", t=PACK, e=2),
                 in_=b_raw[g][:].bitcast(I32).rearrange("p k (v t e) -> p k t v e", t=PACK, e=2),
             )
-            src = b_plane_raw[i][:, :, (g - g0) * PASS : (g - g0 + 1) * PASS]
             nc.vector.tensor_copy(
                 out=b_plane[g][:].bitcast(I32).rearrange("p k (t v) -> p k v t", t=PACK),
-                in_=src.bitcast(I32).rearrange("p k (v t) -> p k v t", t=PACK),
-            )
-
-        rates, rates_packed, h_codes, h_plane, g_packed, acc, scaled = {}, {}, {}, {}, {}, {}, {}
-
-        def stage1(c, g, between):
-            m0, w = CHUNKS[c]
-            rates[c, g] = work.tile([P, PACK, w], BF16, name="rates", tag="rates%d" % c, align_bytes=64)
-            per_bank = 512 // w
-            n = 512 if w == 512 else 128
-            for t0 in range(0, PACK, per_bank):
-                bank = ring.tile([P, per_bank, w], F32, name="bank", tag="ring")
-                for t in range(t0, t0 + per_bank):
-                    for h in range(0, w, n):
-                        for k in range(K_PASSES):
-                            nc.tensor.matmul_mx(
-                                out=bank[:, t - t0, h : h + n],
-                                lhsT=b_codes[g][:, k, 2 * P * t : 2 * P * (t + 1)].bitcast(FP4X4),
-                                lhsT_scale=b_plane[g][:, k, P * t : P * (t + 1)],
-                                rhs=x_codes[c][:, k, h : h + n].bitcast(FP8X4),
-                                rhs_scale=x_plane[:, k, m0 + h : m0 + h + n],
-                                start=(k == 0),
-                                stop=(k == K_PASSES - 1),
-                            )
-                for t in range(t0, t0 + per_bank):
-                    nc.scalar.activation(
-                        out=rates[c, g][:, t, :], in_=bank[:, t - t0, :], func=ACT.Exp, bias=ln_w[:, t, g : g + 1]
-                    )
-                    if t == 0:
-                        between()
-
-        def pack_rates(c, g, copy, lo, hi):
-            if (c, g) not in rates_packed:
-                rates_packed[c, g] = work.tile(
-                    [P, CHUNKS[c][1], PACK], BF16, name="rates_packed", tag="packed%d" % c, align_bytes=64
-                )
-            if lo < hi:
-                copy(
-                    out=rates_packed[c, g][:, lo:hi, :].rearrange("p (a i) t -> p a t i", i=4),
-                    in_=rates[c, g][:, :, lo:hi].rearrange("p t (a i) -> p a t i", i=4),
-                )
-
-        def quantize_rates(c, g):
-            w = CHUNKS[c][1]
-            h_codes[c, g] = kept([P, w], U32, "h_codes%d_%d" % (c, g))
-            h_plane[c, g] = kept([P, w], U8, "h_plane%d_%d" % (c, g))
-            nc.vector.quantize_mx(
-                out=h_codes[c, g][:].bitcast(FP8X4),
-                scales=h_plane[c, g][:],
-                in_=rates_packed[c, g][:].rearrange("p m t -> p (m t)"),
+                in_=raw_scales.bitcast(I32).rearrange("p k (v t) -> p k v t", t=PACK),
             )
 
         def sign_g(g):
             for t in range(PACK):
                 nc.vector.tensor_scalar(
-                    out=g_raw[g][:, t, :], in0=g_raw[g][:, t, :], scalar1=w_sign[:, t, g : g + 1], scalar2=None, op0=ALU.mult
+                    out=g_raw[g][:, t, :],
+                    in0=g_raw[g][:, t, :],
+                    scalar1=w_sign[:, t, g : g + 1],
+                    scalar2=None,
+                    op0=ALU.mult,
                 )
 
         def pack_g(g):
@@ -255,11 +169,57 @@ def tile_weighted_region_expected_events_h2_kernel(
                 in_=g_packed[g][:].rearrange("p s a t -> p (s a t)"),
             )
 
-        def stage2(c, g):
+        def stage1(c, g):
+            m0, w = CHUNKS[c]
+            rates[c, g] = work.tile(
+                [P, PACK, w], BF16, name="rates", tag="rates%d" % c, bufs=(3, GROUPS)[c], align_bytes=64
+            )
+            per_bank = BANK // w
+            n = STAGE1_N[c]
+            for t0 in range(0, PACK, per_bank):
+                bank = ring.tile([P, per_bank, w], F32, name="bank", tag="ring")
+                for t in range(t0, t0 + per_bank):
+                    for col in range(0, w, n):
+                        for k in range(K_PASSES):
+                            nc.tensor.matmul_mx(
+                                out=bank[:, t - t0, col : col + n],
+                                lhsT=b_codes[g][:, k, 2 * P * t : 2 * P * (t + 1)].bitcast(FP4X4),
+                                lhsT_scale=b_plane[g][:, k, P * t : P * (t + 1)],
+                                rhs=x_codes[c][:, k, col : col + n].bitcast(FP8X4),
+                                rhs_scale=x_plane[:, k, m0 + col : m0 + col + n],
+                                start=(k == 0),
+                                stop=(k == K_PASSES - 1),
+                            )
+                for t in range(t0, t0 + per_bank):
+                    nc.scalar.activation(
+                        out=rates[c, g][:, t, :], in_=bank[:, t - t0, :], func=ACT.Exp, bias=ln_w[:, t, g : g + 1]
+                    )
+
+        def pack_rates(c, g, copy, lo, hi):
+            if (c, g) not in rates_packed:
+                rates_packed[c, g] = work.tile(
+                    [P, CHUNKS[c][1], PACK], BF16, name="rates_packed", tag="rates_packed%d" % c, align_bytes=64
+                )
+            if lo < hi:
+                copy(
+                    out=rates_packed[c, g][:, lo:hi, :].rearrange("p (a i) t -> p a t i", i=RUN),
+                    in_=rates[c, g][:, :, lo:hi].rearrange("p t (a i) -> p a t i", i=RUN),
+                )
+
+        def quantize_rates(c, g):
             w = CHUNKS[c][1]
+            h_codes[c, g] = kept([P, w], U32, "h_codes%d_%d" % (c, g))
+            h_plane[c, g] = kept([P, w], U8, "h_plane%d_%d" % (c, g))
+            nc.vector.quantize_mx(
+                out=h_codes[c, g][:].bitcast(FP8X4),
+                scales=h_plane[c, g][:],
+                in_=rates_packed[c, g][:].rearrange("p m t -> p (m t)"),
+            )
+
+        def stage2(c, g):
             for s in range(PACK):
                 if g == 0:
-                    acc[c, s] = sums.tile([P, w], F32, name="acc", tag="acc%d" % s)
+                    acc[c, s] = sums.tile([P, CHUNKS[c][1]], F32, name="acc", tag="acc%d" % s)
                 nc.tensor.matmul_mx(
                     out=acc[c, s][:],
                     lhsT=g_codes[g][:, P * s : P * (s + 1)].bitcast(FP8X4),
@@ -267,158 +227,217 @@ def tile_weighted_region_expected_events_h2_kernel(
                     rhs=h_codes[c, g][:].bitcast(FP8X4),
                     rhs_scale=h_plane[c, g][:],
                     start=(g == 0),
-                    stop=(g == F_PASSES - 1),
+                    stop=(g == GROUPS - 1),
                 )
 
-        def drain(c, on_vector):
-            w = CHUNKS[c][1]
-            scaled[c] = kept([P, PACK, w], F32, "scaled%d" % c)
+        def drain(c):
+            scaled[c] = kept([P, PACK, CHUNKS[c][1]], F32, "scaled%d" % c)
             for s in range(PACK):
-                if s in on_vector:
+                if s % 2 == c:
                     nc.vector.tensor_scalar(
-                        out=scaled[c][:, s, :], in0=acc[c, s][:], scalar1=bg[:, s : s + 1], scalar2=cal[:, s : s + 1],
-                        op0=ALU.add, op1=ALU.mult,
+                        out=scaled[c][:, s, :],
+                        in0=acc[c, s][:],
+                        scalar1=bg[:, s : s + 1],
+                        scalar2=cal[:, s : s + 1],
+                        op0=ALU.add,
+                        op1=ALU.mult,
                     )
                 else:
                     nc.scalar.activation(
-                        out=scaled[c][:, s, :], in_=acc[c, s][:], func=ACT.Identity,
-                        scale=cal[:, s : s + 1], bias=bg_cal[:, s : s + 1],
+                        out=scaled[c][:, s, :],
+                        in_=acc[c, s][:],
+                        func=ACT.Identity,
+                        scale=cal[:, s : s + 1],
+                        bias=bg_cal[:, s : s + 1],
                     )
-
-        y_packed = {}
 
         def pack_y(c, lo, hi):
             m0, w = CHUNKS[c]
             if c not in y_packed:
                 y_packed[c] = kept([P, w, PACK], BF16, "y_packed%d" % c)
+            rt = rt_along_free[:, m0 + lo : m0 + hi].rearrange("p (a i) -> p a i", i=RUN)
             nc.vector.tensor_tensor(
-                out=y_packed[c][:, lo:hi, :].rearrange("p (a i) s -> p a s i", i=4),
-                in0=scaled[c][:, :, lo:hi].rearrange("p s (a i) -> p a s i", i=4),
-                in1=rt_row[:, m0 + lo : m0 + hi]
-                .rearrange("p (a i) -> p a i", i=4)
-                .unsqueeze(2)
-                .to_broadcast([P, (hi - lo) // 4, PACK, 4]),
+                out=y_packed[c][:, lo:hi, :].rearrange("p (a i) s -> p a s i", i=RUN),
+                in0=scaled[c][:, :, lo:hi].rearrange("p s (a i) -> p a s i", i=RUN),
+                in1=rt.unsqueeze(2).to_broadcast([P, (hi - lo) // RUN, PACK, RUN]),
                 op=ALU.mult,
             )
 
-        def turn_rt():
-            bank = ring.tile([P, P], F32, name="bank", tag="ring")
-            nc.tensor.transpose(bank[:], rt_rows32[:], ident[:])
-            nc.vector.tensor_copy(out=rt_col[:], in_=bank[:, 0 : M // P])
-
-        def store_planes(c):
+        def store_planes(c, plane_queue):
             m0, w = CHUNKS[c]
             y_codes = kept([P, w], U32, "y_codes%d" % c)
             y_plane = kept([P, w], U8, "y_plane%d" % c)
             nc.vector.quantize_mx(
                 out=y_codes[:].bitcast(FP8X4), scales=y_plane[:], in_=y_packed[c][:].rearrange("p m s -> p (m s)")
             )
-            dst = out_1[0].rearrange("p m t -> p (m t)")[:, PACK * m0 : PACK * (m0 + w)]
+            dst = out_1[0].rearrange("p m s -> p (m s)")[:, PACK * m0 : PACK * (m0 + w)]
             nc.sync.dma_start(out=dst.bitcast(I32), in_=y_codes[:].bitcast(I32))
-            for q in range(4):
-                nc.sync.dma_start(
+            for q in range(QUADRANTS):
+                plane_queue.dma_start(
                     out=out_2[0, 4 * q : 4 * q + 4, m0 : m0 + w].bitcast(I32),
                     in_=y_plane[32 * q : 32 * q + 4, :].bitcast(I32),
                 )
 
-        def store_y(c, j):
-            m0 = CHUNKS[c][0]
+        def store_y(c, j, on_vector):
             bank = ring.tile([P, PACK, P], F32, name="bank", tag="ring")
             for s in range(PACK):
                 nc.tensor.transpose(bank[:, s, :], scaled[c][:, s, P * j : P * (j + 1)], ident[:])
-            row = m0 // P + j
+            row = CHUNKS[c][0] // P + j
             y = kept([P, P, PACK], F32, "y%d" % row)
-            if row in Y_V:
-                nc.vector.tensor_scalar(
-                    out=y[:], in0=bank[:].rearrange("m s p -> m p s"), scalar1=rt_col[:, row : row + 1], scalar2=None, op0=ALU.mult
-                )
+            turned = bank[:].rearrange("m s p -> m p s")
+            rt = rt_on_partitions[:, row : row + 1]
+            if on_vector:
+                nc.vector.tensor_scalar(out=y[:], in0=turned, scalar1=rt, scalar2=None, op0=ALU.mult)
             else:
-                nc.scalar.activation(
-                    out=y[:], in_=bank[:].rearrange("m s p -> m p s"), func=ACT.Copy, scale=rt_col[:, row : row + 1]
-                )
+                nc.scalar.activation(out=y[:], in_=turned, func=ACT.Copy, scale=rt)
             nc.sync.dma_start(out=out_0[P * row : P * (row + 1), :], in_=y[:].rearrange("m p s -> m (p s)"))
 
-        units = []
-        for g in range(F_PASSES):
-            if FIRST_NARROW and g < EARLY_NARROW:
-                units.append((1, g))
-            units.append((0, g))
-            if not FIRST_NARROW and 1 <= g <= EARLY_NARROW:
-                units.append((1, g - 1))
-        last_wide = units.index((0, F_PASSES - 1))
-        units += [(1, g) for g in range(EARLY_NARROW, F_PASSES)]
+        def warm_up(passes):
+            idle = sums.tile([P, P], F32, name="idle", tag="acc0")
+            for n in range(passes):
+                nc.tensor.matmul_mx(
+                    out=idle[:],
+                    lhsT=zero_codes[:].bitcast(FP8X4),
+                    lhsT_scale=zero_plane[:],
+                    rhs=zero_codes[:].bitcast(FP8X4),
+                    rhs_scale=zero_plane[:],
+                    start=True,
+                    stop=True,
+                )
 
+        nc.vector.memset(b_plane_raw[0][:].bitcast(I32), 0)
+        nc.vector.memset(x_plane[:].bitcast(I32), 0)
+        nc.vector.memset(zeros[:], 0.0)
+        nc.vector.memset(one[:], 1.0)
+        nc.vector.memset(w_rows32[:], 0.0)
+        nc.vector.quantize_mx(out=zero_codes[:].bitcast(FP8X4), scales=zero_plane[:], in_=zeros[:])
+        make_identity(nc, ident[:])
+        for plane in b_plane_raw[1:]:
+            nc.vector.memset(plane[:].bitcast(I32), 0)
+
+        nc.scalar.dma_start(out=w_rows[0:GROUPS, :], in_=age_w.rearrange("(g f) -> g f", f=PASS))
+        nc.scalar.activation(out=unused[:], in_=one[:], func=ACT.Ln)
+
+        for item in LOADS.split():
+            if item == "p":
+                load_plane(x_plane, x_scales)
+            elif item == "r":
+                nc.sync.dma_start(out=rt_rows[0 : M // P, :], in_=risk_time.rearrange("(j p) -> j p", p=P))
+            elif item == "c":
+                load_epilogue_vectors()
+            else:
+                {"b": load_b, "x": load_x, "s": load_b_plane, "g": load_g}[item[0]](int(item[1]))
+
+        warm_up(WARM_PASSES[0])
+        nc.vector.tensor_copy(
+            out=w_rows32[0:GROUPS, :, :].rearrange("g t (v r) -> g t v r", r=4),
+            in_=w_rows[0:GROUPS, :].rearrange("g (v t r) -> g t v r", t=PACK, r=4),
+        )
+        w_turned = ring.tile([P, PACK, P], F32, name="w_turned", tag="ring")
+        for t in range(PACK):
+            nc.tensor.transpose(w_turned[:, t, :], w_rows32[:, t, :], ident[:])
+        warm_up(WARM_PASSES[1])
         order_b(0)
+        nc.vector.tensor_copy(out=w_col[:], in_=w_turned[:, :, 0:GROUPS])
+
+        w_bits = w_col[:].bitcast(I32)
+        nc.vector.tensor_scalar(
+            out=w_frac[:], in0=w_bits, scalar1=16, scalar2=127, op0=ALU.logical_shift_right, op1=ALU.bitwise_and
+        )
+        nc.vector.tensor_scalar(
+            out=w_expo[:], in0=w_bits, scalar1=23, scalar2=255, op0=ALU.logical_shift_right, op1=ALU.bitwise_and
+        )
+        nc.vector.tensor_scalar(
+            out=w_mant[:], in0=w_frac[:], scalar1=1.0 / 128, scalar2=1.0, op0=ALU.mult, op1=ALU.add
+        )
+        nc.scalar.activation(out=ln_mant[:], in_=w_mant[:], func=ACT.Ln)
+        nc.scalar.activation(out=unused[:], in_=one[:], func=ACT.Exp)
+        nc.vector.tensor_scalar(
+            out=ln_expo[:], in0=w_expo[:], scalar1=-127.0, scalar2=math.log(2.0), op0=ALU.add, op1=ALU.mult
+        )
+        nc.vector.tensor_scalar(
+            out=ln_zero[:], in0=w_expo[:], scalar1=0.0, scalar2=ZERO_WEIGHT_LOG, op0=ALU.is_equal, op1=ALU.mult
+        )
+        nc.vector.tensor_scalar(out=w_neg[:], in0=w_col[:], scalar1=0.0, scalar2=-2.0, op0=ALU.is_lt, op1=ALU.mult)
         nc.vector.tensor_tensor(out=ln_rest[:], in0=ln_expo[:], in1=ln_zero[:], op=ALU.add)
         nc.vector.tensor_scalar(out=w_sign[:], in0=w_neg[:], scalar1=1.0, scalar2=None, op0=ALU.add)
         nc.vector.tensor_tensor(out=ln_w[:], in0=ln_rest[:], in1=ln_mant[:], op=ALU.add)
         order_b(1)
 
         fillers = []
-        for g in range(F_PASSES + 1):
-            if g < F_PASSES:
+        for g in range(GROUPS + 1):
+            if g < GROUPS:
                 fillers.append((sign_g, g))
             if g >= 1:
                 fillers.append((quantize_g, g - 1))
-            if g + 2 < F_PASSES:
-                fillers.append((order_b, g + 2))
-            if g < F_PASSES:
+            if g < GROUPS:
                 fillers.append((pack_g, g))
+            if g + 2 < GROUPS:
+                fillers.append((order_b, g + 2))
 
         def fill(count):
-            for step, g in fillers[:count]:
-                step(g)
+            for piece, g in fillers[:count]:
+                piece(g)
             fillers[:count] = []
 
-        narrow_done = 0
-        fill(FILL_LEAD)
-        for i in range(len(units) + 2):
-            now = units[i] if i < len(units) else None
-            prev = units[i - 1] if 1 <= i <= len(units) else None
-            prev2 = units[i - 2] if i >= 2 else None
-            share = (SCALAR_SHARE if i < last_wide + LATE_FROM else LATE_SHARE)[prev[0]] if prev else 0
+        wide_units = [(WIDE, g) for g in range(GROUPS)]
+        narrow_units = [(NARROW, g) for g in range(GROUPS)]
+        units = (
+            wide_units[:EARLY_WIDE] + narrow_units[:EARLY_NARROW] + wide_units[EARLY_WIDE:] + narrow_units[EARLY_NARROW:]
+        )
+        pack_step = {u: NARROW_PACK_STEP[u[1]] if u[0] == NARROW else i + 1 for i, u in enumerate(units)}
+        last_wide = units.index((WIDE, GROUPS - 1))
+        wide_done = WIDE_STAGE2_STEP[-1]
+        half = CHUNKS[WIDE][1] // 2
+        narrow_next = 0
+        fill(FILL_AHEAD)
+        for i in range(STEPS):
+            for g in range(GROUPS):
+                if WIDE_STAGE2_STEP[g] == i:
+                    stage2(WIDE, g)
+            if i == wide_done:
+                drain(WIDE)
+            if i < len(units):
+                stage1(*units[i])
+            to_pack = [u for u in units if pack_step[u] == i]
+            for c, g in to_pack:
+                pack_rates(c, g, nc.scalar.copy, 0, SCALAR_COLUMNS[c][g])
+            for c, g in to_pack:
+                pack_rates(c, g, nc.vector.tensor_copy, SCALAR_COLUMNS[c][g], CHUNKS[c][1])
+            fill(1)
+            for u in units:
+                if pack_step[u] + 1 == i:
+                    quantize_rates(*u)
+            fill(1)
 
-            def scalar_share():
-                if prev:
-                    pack_rates(*prev, nc.scalar.copy, 0, share)
-
-            if now:
-                stage1(*now, scalar_share)
-            else:
-                scalar_share()
-            count = FILL_RATE[now[0]] if now else 0
-            if prev:
-                pack_rates(*prev, nc.vector.tensor_copy, share, CHUNKS[prev[0]][1])
-            fill((count + 1) // 2)
-            if prev:
-                quantize_rates(*prev)
-            fill(count // 2)
             if i == last_wide:
                 nc.vector.tensor_copy(out=cal[:], in_=cal_bf[:])
                 nc.vector.tensor_copy(out=bg[:], in_=bg_bf[:])
-                nc.vector.tensor_copy(out=rt_rows32[0 : M // P, :], in_=rt_rows[0 : M // P, :])
                 nc.vector.tensor_tensor(out=bg_cal[:], in0=cal_bf[:], in1=bg_bf[:], op=ALU.mult)
-            if prev2 and prev2[0] == 0:
-                stage2(*prev2)
-            if i == last_wide + 2:
-                drain(0, DRAIN_V[0])
-            for j in range(2):
-                if i == last_wide + PY_STEPS[j]:
-                    pack_y(0, 256 * j, 256 * (j + 1))
-            if i == last_wide + PL_STEP:
-                store_planes(0)
-            if i == last_wide + Y_STEPS[0]:
-                turn_rt()
-            for j in range(4):
-                if i == last_wide + Y_STEPS[j]:
-                    store_y(0, j)
-            if i >= last_wide + 2:
-                ready = [g for g in range(narrow_done, F_PASSES) if (1, g) in units[: i - 1]]
-                for g in ready if i == len(units) + 1 else ready[:CATCH]:
-                    stage2(1, g)
-                    narrow_done += 1
-        drain(1, DRAIN_V[1])
-        pack_y(1, 0, 256)
-        for j in range(2):
-            store_y(1, j)
-        store_planes(1)
+            if i == RISK_STEP - 2:
+                nc.vector.memset(rt_rows32[:], 0.0)
+            if i == RISK_STEP - 1:
+                nc.vector.tensor_copy(out=rt_rows32[0 : M // P, :], in_=rt_rows[0 : M // P, :])
+            if i == RISK_STEP:
+                rt_turned = ring.tile([P, P], F32, name="rt_turned", tag="ring")
+                nc.tensor.transpose(rt_turned[:], rt_rows32[:], ident[:])
+                nc.vector.tensor_copy(out=rt_on_partitions[:], in_=rt_turned[:, 0 : M // P])
+
+            if i == wide_done + 1:
+                pack_y(WIDE, 0, half)
+                for j in range(CHUNKS[WIDE][1] // P):
+                    store_y(WIDE, j, False)
+            if i == STEPS - 1:
+                pack_y(WIDE, half, 2 * half)
+                store_planes(WIDE, nc.sync)
+            if i >= wide_done:
+                for g in range(narrow_next, min(narrow_next + NARROW_PASSES_A_STEP, GROUPS)):
+                    if (NARROW, g) in h_codes:
+                        stage2(NARROW, g)
+                        narrow_next = g + 1
+
+        drain(NARROW)
+        pack_y(NARROW, 0, CHUNKS[NARROW][1])
+        store_y(NARROW, 0, False)
+        store_y(NARROW, 1, True)
+        store_planes(NARROW, nc.scalar)

@@ -75,8 +75,6 @@ def tile_weighted_region_expected_events_h2_kernel(
         rt_rows = kept([P, P], BF16, "rt_rows")
         rt_rows32 = kept([P, P], F32, "rt_rows32")
         ident = kept([P, P], F32, "ident")
-        one = kept([P, 1], F32, "one")
-        unused = kept([P, 1], F32, "unused")
         cal_bf = kept([P, PACK], BF16, "cal_bf")
         bg_bf = kept([P, PACK], BF16, "bg_bf")
         cal = kept([P, PACK], F32, "cal")
@@ -308,7 +306,6 @@ def tile_weighted_region_expected_events_h2_kernel(
         nc.vector.memset(b_plane_raw[0][:].bitcast(I32), 0)
         nc.vector.memset(x_plane[:].bitcast(I32), 0)
         nc.vector.memset(zeros[:], 0.0)
-        nc.vector.memset(one[:], 1.0)
         nc.vector.memset(w_rows32[:], 0.0)
         nc.vector.quantize_mx(out=zero_codes[:].bitcast(FP8X4), scales=zero_plane[:], in_=zeros[:])
         make_identity(nc, ident[:])
@@ -316,7 +313,6 @@ def tile_weighted_region_expected_events_h2_kernel(
             nc.vector.memset(plane[:].bitcast(I32), 0)
 
         nc.scalar.dma_start(out=w_rows[0:GROUPS, :], in_=age_w.rearrange("(g f) -> g f", f=PASS))
-        nc.scalar.activation(out=unused[:], in_=one[:], func=ACT.Ln)
 
         for item in LOADS.split():
             if item == "p":
@@ -351,7 +347,6 @@ def tile_weighted_region_expected_events_h2_kernel(
             out=w_mant[:], in0=w_frac[:], scalar1=1.0 / 128, scalar2=1.0, op0=ALU.mult, op1=ALU.add
         )
         nc.scalar.activation(out=ln_mant[:], in_=w_mant[:], func=ACT.Ln)
-        nc.scalar.activation(out=unused[:], in_=one[:], func=ACT.Exp)
         nc.vector.tensor_scalar(
             out=ln_expo[:], in0=w_expo[:], scalar1=-127.0, scalar2=math.log(2.0), op0=ALU.add, op1=ALU.mult
         )

import math
from contextlib import ExitStack

import concourse.mybir as mybir
from concourse.masks import make_identity

M, K, F, N = 768, 1024, 4096, 512
FLOPS = 2 * M * K * F + 2 * M * F * N

F32 = mybir.dt.float32
BF16 = mybir.dt.bfloat16
I32 = mybir.dt.int32
U32 = mybir.dt.uint32
U8 = mybir.dt.uint8
FP8X4 = mybir.dt.float8_e4m3fn_x4
FP4X4 = mybir.dt.float4_e2m1fn_x4
ALU = mybir.AluOpType
ACT = mybir.ActivationFunctionType

P = 128
PACK = 4
PASS = P * PACK
BANK = 512
RUN = 4
QUADRANTS = 4
K_PASSES = K // PASS
GROUPS = F // PASS
WIDE, NARROW = 0, 1
CHUNKS = ((0, 512), (512, 256))
STAGE1_N = (512, 128)
ZERO_WEIGHT_LOG = -1.0e30

B_PLANE_PARTS = ((0, 2), (2, 3), (5, 3))
LOADS = "b0 s0 x0 p b1 g0 s1 b2 g1 x1 r b3 g2 s2 b4 g3 b5 g4 c b6 g5 b7 g6 g7"

EARLY_WIDE, EARLY_NARROW = 3, 4
NARROW_PACK_STEP = (11, 12, 13, 14, 14, 15, 16, 17)
WIDE_STAGE2_STEP = (6, 9, 10, 11, 12, 14, 15, 15)
SCALAR_COLUMNS = ((128, 128, 256, 256, 256, 256, 256, 256), (64, 64, 64, 64, 0, 0, 0, 0))
FILL_AHEAD = 3
RISK_STEP = 10
NARROW_PASSES_A_STEP = 4
STEPS = 19
WARM_PASSES = (5, 14)


def tile_weighted_region_expected_events_h2_kernel(
    tc, x_words, x_scales, b_words, b_scales, age_w, group_w, background, calibration, risk_time, out_0, out_1, out_2
):
    nc = tc.nc
    with ExitStack() as ctx:
        keep = ctx.enter_context(tc.tile_pool(name="keep", bufs=1))
        work = ctx.enter_context(tc.tile_pool(name="work", bufs=3))
        ring = ctx.enter_context(tc.psum_pool(name="ring", bufs=4))
        sums = ctx.enter_context(tc.psum_pool(name="sums", bufs=1))
        ctx.enter_context(tc.manual_schedule())

        def kept(shape, dtype, name):
            return keep.tile(shape, dtype, name=name, align_bytes=64)

        def per_cell(dtype, name):
            return kept([P, PACK, GROUPS], dtype, name)

        x_codes = [kept([P, K_PASSES, w], U32, "x_codes%d" % c) for c, (m0, w) in enumerate(CHUNKS)]
        x_plane = kept([P, K_PASSES, M], U8, "x_plane")
        b_plane_raw = [
            kept([P, K_PASSES, n * PASS], U8, "b_plane_raw%d" % i) for i, (g0, n) in enumerate(B_PLANE_PARTS)
        ]
        b_plane = [kept([P, K_PASSES, PASS], U8, "b_plane%d" % g) for g in range(GROUPS)]
        b_codes = [kept([P, K_PASSES, 2 * PASS], U8, "b_codes%d" % g) for g in range(GROUPS)]
        g_codes = [kept([P, N], U32, "g_codes%d" % g) for g in range(GROUPS)]
        g_plane = [kept([P, N], U8, "g_plane%d" % g) for g in range(GROUPS)]
        w_rows = kept([P, PASS], BF16, "w_rows")
        w_rows32 = kept([P, PACK, P], F32, "w_rows32")
        rt_rows = kept([P, P], BF16, "rt_rows")
        rt_rows32 = kept([P, P], F32, "rt_rows32")
        ident = kept([P, P], F32, "ident")
        cal_bf = kept([P, PACK], BF16, "cal_bf")
        bg_bf = kept([P, PACK], BF16, "bg_bf")
        cal = kept([P, PACK], F32, "cal")
        bg = kept([P, PACK], F32, "bg")
        bg_cal = kept([P, PACK], F32, "bg_cal")
        rt_along_free = kept([P, M], BF16, "rt_along_free")
        rt_on_partitions = kept([P, M // P], F32, "rt_on_partitions")
        w_col = per_cell(F32, "w_col")
        w_expo = per_cell(I32, "w_expo")
        w_frac = per_cell(I32, "w_frac")
        w_mant = per_cell(F32, "w_mant")
        ln_mant = per_cell(F32, "ln_mant")
        ln_expo = per_cell(F32, "ln_expo")
        ln_zero = per_cell(F32, "ln_zero")
        ln_rest = per_cell(F32, "ln_rest")
        ln_w = per_cell(F32, "ln_w")
        w_neg = per_cell(F32, "w_neg")
        w_sign = per_cell(F32, "w_sign")
        zeros = kept([P, PASS], BF16, "zeros")
        zero_codes = kept([P, P], U32, "zero_codes")
        zero_plane = kept([P, P], U8, "zero_plane")
        b_raw, g_raw, g_packed = {}, {}, {}
        rates, rates_packed, h_codes, h_plane = {}, {}, {}, {}
        acc, scaled, y_packed = {}, {}, {}

        def load_x(c):
            m0, w = CHUNKS[c]
            src = x_words.rearrange("k p m t -> p k (m t)")[:, :, PACK * m0 : PACK * (m0 + w)]
            nc.sync.dma_start(out=x_codes[c][:].bitcast(I32), in_=src.bitcast(I32))

        def load_plane(plane, scales):
            for q in range(QUADRANTS):
                src = scales[:, 4 * q : 4 * q + 4, :].rearrange("k r n -> r k n")
                nc.sync.dma_start(out=plane[32 * q : 32 * q + 4, :, :].bitcast(I32), in_=src.bitcast(I32))

        def load_b_plane(i):
            g0, n = B_PLANE_PARTS[i]
            load_plane(b_plane_raw[i], b_scales[:, :, g0 * PASS : (g0 + n) * PASS])

        def load_b(g):
            b_raw[g] = work.tile([P, K_PASSES, 2 * PASS], U8, name="b_raw", bufs=4, align_bytes=64)
            src = b_words.rearrange("k p n -> p k n")[:, :, 2 * PASS * g : 2 * PASS * (g + 1)]
            nc.sync.dma_start(out=b_raw[g][:].bitcast(I32), in_=src.bitcast(I32))

        def load_g(g):
            g_raw[g] = work.tile([P, PACK, N], BF16, name="g_raw", bufs=6, align_bytes=64)
            src = group_w[PASS * g : PASS * (g + 1), :].rearrange("(v t r) n -> r v t n", t=PACK, r=4)
            for r in range(4):
                nc.sync.dma_start(out=g_raw[g][r:P:4, :, :], in_=src[r])

        def load_epilogue_vectors():
            nc.sync.dma_start(out=cal_bf[:], in_=calibration.rearrange("(p s) -> p s", s=PACK))
            nc.sync.dma_start(out=bg_bf[:], in_=background.rearrange("(p s) -> p s", s=PACK))
            nc.sync.dma_start(out=rt_along_free[:], in_=risk_time.partition_broadcast(P))

        def order_b(g):
            part = max(i for i, (g0, n) in enumerate(B_PLANE_PARTS) if g0 <= g)
            first = (g - B_PLANE_PARTS[part][0]) * PASS
            raw_scales = b_plane_raw[part][:, :, first : first + PASS]
            nc.vector.tensor_copy(
                out=b_codes[g][:].bitcast(I32).rearrange("p k (t v e) -> p k t v e", t=PACK, e=2),
                in_=b_raw[g][:].bitcast(I32).rearrange("p k (v t e) -> p k t v e", t=PACK, e=2),
            )
            nc.vector.tensor_copy(
                out=b_plane[g][:].bitcast(I32).rearrange("p k (t v) -> p k v t", t=PACK),
                in_=raw_scales.bitcast(I32).rearrange("p k (v t) -> p k v t", t=PACK),
            )

        def sign_g(g):
            for t in range(PACK):
                nc.vector.tensor_scalar(
                    out=g_raw[g][:, t, :],
                    in0=g_raw[g][:, t, :],
                    scalar1=w_sign[:, t, g : g + 1],
                    scalar2=None,
                    op0=ALU.mult,
                )

        def pack_g(g):
            g_packed[g] = work.tile([P, PACK, P, PACK], BF16, name="g_packed", align_bytes=64)
            nc.vector.tensor_copy(
                out=g_packed[g][:].rearrange("p s a t -> p a t s"),
                in_=g_raw[g][:].rearrange("p t (a s) -> p a t s", s=PACK),
            )

        def quantize_g(g):
            nc.vector.quantize_mx(
                out=g_codes[g][:].bitcast(FP8X4),
                scales=g_plane[g][:],
                in_=g_packed[g][:].rearrange("p s a t -> p (s a t)"),
            )

        def stage1(c, g):
            m0, w = CHUNKS[c]
            rates[c, g] = work.tile(
                [P, PACK, w], BF16, name="rates", tag="rates%d" % c, bufs=(3, GROUPS)[c], align_bytes=64
            )
            per_bank = BANK // w
            n = STAGE1_N[c]
            for t0 in range(0, PACK, per_bank):
                bank = ring.tile([P, per_bank, w], F32, name="bank", tag="ring")
                for t in range(t0, t0 + per_bank):
                    for col in range(0, w, n):
                        for k in range(K_PASSES):
                            nc.tensor.matmul_mx(
                                out=bank[:, t - t0, col : col + n],
                                lhsT=b_codes[g][:, k, 2 * P * t : 2 * P * (t + 1)].bitcast(FP4X4),
                                lhsT_scale=b_plane[g][:, k, P * t : P * (t + 1)],
                                rhs=x_codes[c][:, k, col : col + n].bitcast(FP8X4),
                                rhs_scale=x_plane[:, k, m0 + col : m0 + col + n],
                                start=(k == 0),
                                stop=(k == K_PASSES - 1),
                            )
                for t in range(t0, t0 + per_bank):
                    nc.scalar.activation(
                        out=rates[c, g][:, t, :], in_=bank[:, t - t0, :], func=ACT.Exp, bias=ln_w[:, t, g : g + 1]
                    )

        def pack_rates(c, g, copy, lo, hi):
            if (c, g) not in rates_packed:
                rates_packed[c, g] = work.tile(
                    [P, CHUNKS[c][1], PACK], BF16, name="rates_packed", tag="rates_packed%d" % c, align_bytes=64
                )
            if lo < hi:
                copy(
                    out=rates_packed[c, g][:, lo:hi, :].rearrange("p (a i) t -> p a t i", i=RUN),
                    in_=rates[c, g][:, :, lo:hi].rearrange("p t (a i) -> p a t i", i=RUN),
                )

        def quantize_rates(c, g):
            w = CHUNKS[c][1]
            h_codes[c, g] = kept([P, w], U32, "h_codes%d_%d" % (c, g))
            h_plane[c, g] = kept([P, w], U8, "h_plane%d_%d" % (c, g))
            nc.vector.quantize_mx(
                out=h_codes[c, g][:].bitcast(FP8X4),
                scales=h_plane[c, g][:],
                in_=rates_packed[c, g][:].rearrange("p m t -> p (m t)"),
            )

        def stage2(c, g):
            for s in range(PACK):
                if g == 0:
                    acc[c, s] = sums.tile([P, CHUNKS[c][1]], F32, name="acc", tag="acc%d" % s)
                nc.tensor.matmul_mx(
                    out=acc[c, s][:],
                    lhsT=g_codes[g][:, P * s : P * (s + 1)].bitcast(FP8X4),
                    lhsT_scale=g_plane[g][:, P * s : P * (s + 1)],
                    rhs=h_codes[c, g][:].bitcast(FP8X4),
                    rhs_scale=h_plane[c, g][:],
                    start=(g == 0),
                    stop=(g == GROUPS - 1),
                )

        def drain(c):
            scaled[c] = kept([P, PACK, CHUNKS[c][1]], F32, "scaled%d" % c)
            for s in range(PACK):
                if s % 2 == c:
                    nc.vector.tensor_scalar(
                        out=scaled[c][:, s, :],
                        in0=acc[c, s][:],
                        scalar1=bg[:, s : s + 1],
                        scalar2=cal[:, s : s + 1],
                        op0=ALU.add,
                        op1=ALU.mult,
                    )
                else:
                    nc.scalar.activation(
                        out=scaled[c][:, s, :],
                        in_=acc[c, s][:],
                        func=ACT.Identity,
                        scale=cal[:, s : s + 1],
                        bias=bg_cal[:, s : s + 1],
                    )

        def pack_y(c, lo, hi):
            m0, w = CHUNKS[c]
            if c not in y_packed:
                y_packed[c] = kept([P, w, PACK], BF16, "y_packed%d" % c)
            rt = rt_along_free[:, m0 + lo : m0 + hi].rearrange("p (a i) -> p a i", i=RUN)
            nc.vector.tensor_tensor(
                out=y_packed[c][:, lo:hi, :].rearrange("p (a i) s -> p a s i", i=RUN),
                in0=scaled[c][:, :, lo:hi].rearrange("p s (a i) -> p a s i", i=RUN),
                in1=rt.unsqueeze(2).to_broadcast([P, (hi - lo) // RUN, PACK, RUN]),
                op=ALU.mult,
            )

        def store_planes(c, plane_queue):
            m0, w = CHUNKS[c]
            y_codes = kept([P, w], U32, "y_codes%d" % c)
            y_plane = kept([P, w], U8, "y_plane%d" % c)
            nc.vector.quantize_mx(
                out=y_codes[:].bitcast(FP8X4), scales=y_plane[:], in_=y_packed[c][:].rearrange("p m s -> p (m s)")
            )
            dst = out_1[0].rearrange("p m s -> p (m s)")[:, PACK * m0 : PACK * (m0 + w)]
            nc.sync.dma_start(out=dst.bitcast(I32), in_=y_codes[:].bitcast(I32))
            for q in range(QUADRANTS):
                plane_queue.dma_start(
                    out=out_2[0, 4 * q : 4 * q + 4, m0 : m0 + w].bitcast(I32),
                    in_=y_plane[32 * q : 32 * q + 4, :].bitcast(I32),
                )

        def store_y(c, j, on_vector):
            bank = ring.tile([P, PACK, P], F32, name="bank", tag="ring")
            for s in range(PACK):
                nc.tensor.transpose(bank[:, s, :], scaled[c][:, s, P * j : P * (j + 1)], ident[:])
            row = CHUNKS[c][0] // P + j
            y = kept([P, P, PACK], F32, "y%d" % row)
            turned = bank[:].rearrange("m s p -> m p s")
            rt = rt_on_partitions[:, row : row + 1]
            if on_vector:
                nc.vector.tensor_scalar(out=y[:], in0=turned, scalar1=rt, scalar2=None, op0=ALU.mult)
            else:
                nc.scalar.activation(out=y[:], in_=turned, func=ACT.Copy, scale=rt)
            nc.sync.dma_start(out=out_0[P * row : P * (row + 1), :], in_=y[:].rearrange("m p s -> m (p s)"))

        def warm_up(passes):
            idle = sums.tile([P, P], F32, name="idle", tag="acc0")
            for n in range(passes):
                nc.tensor.matmul_mx(
                    out=idle[:],
                    lhsT=zero_codes[:].bitcast(FP8X4),
                    lhsT_scale=zero_plane[:],
                    rhs=zero_codes[:].bitcast(FP8X4),
                    rhs_scale=zero_plane[:],
                    start=True,
                    stop=True,
                )

        nc.vector.memset(b_plane_raw[0][:].bitcast(I32), 0)
        nc.vector.memset(x_plane[:].bitcast(I32), 0)
        nc.vector.memset(zeros[:], 0.0)
        nc.vector.memset(w_rows32[:], 0.0)
        nc.vector.quantize_mx(out=zero_codes[:].bitcast(FP8X4), scales=zero_plane[:], in_=zeros[:])
        make_identity(nc, ident[:])
        for plane in b_plane_raw[1:]:
            nc.vector.memset(plane[:].bitcast(I32), 0)

        nc.scalar.dma_start(out=w_rows[0:GROUPS, :], in_=age_w.rearrange("(g f) -> g f", f=PASS))

        for item in LOADS.split():
            if item == "p":
                load_plane(x_plane, x_scales)
            elif item == "r":
                nc.sync.dma_start(out=rt_rows[0 : M // P, :], in_=risk_time.rearrange("(j p) -> j p", p=P))
            elif item == "c":
                load_epilogue_vectors()
            else:
                {"b": load_b, "x": load_x, "s": load_b_plane, "g": load_g}[item[0]](int(item[1]))

        warm_up(WARM_PASSES[0])
        nc.vector.tensor_copy(
            out=w_rows32[0:GROUPS, :, :].rearrange("g t (v r) -> g t v r", r=4),
            in_=w_rows[0:GROUPS, :].rearrange("g (v t r) -> g t v r", t=PACK, r=4),
        )
        w_turned = ring.tile([P, PACK, P], F32, name="w_turned", tag="ring")
        for t in range(PACK):
            nc.tensor.transpose(w_turned[:, t, :], w_rows32[:, t, :], ident[:])
        warm_up(WARM_PASSES[1])
        order_b(0)
        nc.vector.tensor_copy(out=w_col[:], in_=w_turned[:, :, 0:GROUPS])

        w_bits = w_col[:].bitcast(I32)
        nc.vector.tensor_scalar(
            out=w_frac[:], in0=w_bits, scalar1=16, scalar2=127, op0=ALU.logical_shift_right, op1=ALU.bitwise_and
        )
        nc.vector.tensor_scalar(
            out=w_expo[:], in0=w_bits, scalar1=23, scalar2=255, op0=ALU.logical_shift_right, op1=ALU.bitwise_and
        )
        nc.vector.tensor_scalar(
            out=w_mant[:], in0=w_frac[:], scalar1=1.0 / 128, scalar2=1.0, op0=ALU.mult, op1=ALU.add
        )
        nc.scalar.activation(out=ln_mant[:], in_=w_mant[:], func=ACT.Ln)
        nc.vector.tensor_scalar(
            out=ln_expo[:], in0=w_expo[:], scalar1=-127.0, scalar2=math.log(2.0), op0=ALU.add, op1=ALU.mult
        )
        nc.vector.tensor_scalar(
            out=ln_zero[:], in0=w_expo[:], scalar1=0.0, scalar2=ZERO_WEIGHT_LOG, op0=ALU.is_equal, op1=ALU.mult
        )
        nc.vector.tensor_scalar(out=w_neg[:], in0=w_col[:], scalar1=0.0, scalar2=-2.0, op0=ALU.is_lt, op1=ALU.mult)
        nc.vector.tensor_tensor(out=ln_rest[:], in0=ln_expo[:], in1=ln_zero[:], op=ALU.add)
        nc.vector.tensor_scalar(out=w_sign[:], in0=w_neg[:], scalar1=1.0, scalar2=None, op0=ALU.add)
        nc.vector.tensor_tensor(out=ln_w[:], in0=ln_rest[:], in1=ln_mant[:], op=ALU.add)
        order_b(1)

        fillers = []
        for g in range(GROUPS + 1):
            if g < GROUPS:
                fillers.append((sign_g, g))
            if g >= 1:
                fillers.append((quantize_g, g - 1))
            if g < GROUPS:
                fillers.append((pack_g, g))
            if g + 2 < GROUPS:
                fillers.append((order_b, g + 2))

        def fill(count):
            for piece, g in fillers[:count]:
                piece(g)
            fillers[:count] = []

        wide_units = [(WIDE, g) for g in range(GROUPS)]
        narrow_units = [(NARROW, g) for g in range(GROUPS)]
        units = (
            wide_units[:EARLY_WIDE] + narrow_units[:EARLY_NARROW] + wide_units[EARLY_WIDE:] + narrow_units[EARLY_NARROW:]
        )
        pack_step = {u: NARROW_PACK_STEP[u[1]] if u[0] == NARROW else i + 1 for i, u in enumerate(units)}
        last_wide = units.index((WIDE, GROUPS - 1))
        wide_done = WIDE_STAGE2_STEP[-1]
        half = CHUNKS[WIDE][1] // 2
        narrow_next = 0
        fill(FILL_AHEAD)
        for i in range(STEPS):
            for g in range(GROUPS):
                if WIDE_STAGE2_STEP[g] == i:
                    stage2(WIDE, g)
            if i == wide_done:
                drain(WIDE)
            if i < len(units):
                stage1(*units[i])
            to_pack = [u for u in units if pack_step[u] == i]
            for c, g in to_pack:
                pack_rates(c, g, nc.scalar.copy, 0, SCALAR_COLUMNS[c][g])
            for c, g in to_pack:
                pack_rates(c, g, nc.vector.tensor_copy, SCALAR_COLUMNS[c][g], CHUNKS[c][1])
            fill(1)
            for u in units:
                if pack_step[u] + 1 == i:
                    quantize_rates(*u)
            fill(1)

            if i == last_wide:
                nc.vector.tensor_copy(out=cal[:], in_=cal_bf[:])
                nc.vector.tensor_copy(out=bg[:], in_=bg_bf[:])
                nc.vector.tensor_tensor(out=bg_cal[:], in0=cal_bf[:], in1=bg_bf[:], op=ALU.mult)
            if i == RISK_STEP - 2:
                nc.vector.memset(rt_rows32[:], 0.0)
            if i == RISK_STEP - 1:
                nc.vector.tensor_copy(out=rt_rows32[0 : M // P, :], in_=rt_rows[0 : M // P, :])
            if i == RISK_STEP:
                rt_turned = ring.tile([P, P], F32, name="rt_turned", tag="ring")
                nc.tensor.transpose(rt_turned[:], rt_rows32[:], ident[:])
                nc.vector.tensor_copy(out=rt_on_partitions[:], in_=rt_turned[:, 0 : M // P])

            if i == wide_done + 1:
                pack_y(WIDE, 0, half)
                for j in range(CHUNKS[WIDE][1] // P):
                    store_y(WIDE, j, False)
            if i == STEPS - 1:
                pack_y(WIDE, half, 2 * half)
                store_planes(WIDE, nc.sync)
            if i >= wide_done:
                for g in range(narrow_next, min(narrow_next + NARROW_PASSES_A_STEP, GROUPS)):
                    if (NARROW, g) in h_codes:
                        stage2(NARROW, g)
                        narrow_next = g + 1

        drain(NARROW)
        pack_y(NARROW, 0, CHUNKS[NARROW][1])
        store_y(NARROW, 0, False)
        store_y(NARROW, 1, True)
        store_planes(NARROW, nc.scalar)
